import numpy as np
import ml_dtypes


def mxq(x, axis, fmt="e4m3"):
    dtype, down = {"e4m3": (ml_dtypes.float8_e4m3fn, 7), "e5m2": (ml_dtypes.float8_e5m2, 14)}[fmt]
    v = np.moveaxis(np.asarray(x, np.float32).astype(ml_dtypes.bfloat16).astype(np.float64), axis, -1)
    blocks = v.reshape(v.shape[:-1] + (-1, 32))
    amax = np.abs(blocks).max(-1, keepdims=True)
    byte = np.maximum(np.where(amax > 0, np.frexp(amax)[1] - 1 + 127, 0) - down, 1)
    scale = np.exp2(byte - 127.0)
    codes = (blocks / scale).astype(np.float32).astype(dtype).astype(np.float64)
    return np.moveaxis((codes * scale).reshape(v.shape), -1, axis)


WIDE = False


def mx_kscale(k):
    if not WIDE:
        return np.ones(k)
    levels = np.array([10, -10, 5, -5, 0])
    if k % 512:
        return np.exp2(np.random.permutation(np.resize(levels, k // 32))).repeat(32)
    a = np.empty((k // 512, 16))
    for p in range(k // 512):
        a[p, :8] = np.random.permutation(np.resize(levels, 8))
        for g in range(8):
            far = levels[np.abs(levels - a[p, g]) >= 10]
            a[p, g + 8] = far[np.random.randint(len(far))]
    return np.exp2(a.ravel()).repeat(32)


def f64(x):
    return np.asarray(x).astype(np.float64)


def striped(idx):
    return np.tile(idx.reshape(-1, 16).T, (8, 1)).astype(np.uint16)


def unstriped(offs):
    return offs[:16].T.reshape(-1).astype(np.int64)


K, T, E, C, N = 256, 1024, 6, 512, 128
TOP = 3


def setup_inputs():
    n = np.random.standard_normal
    deal = np.repeat(np.arange(E), C).reshape(TOP, T)[:, np.random.permutation(T)]
    deal = np.take_along_axis(deal, np.argsort(np.random.rand(TOP, T), axis=0), axis=0)
    for _ in range(8):
        s_, t_ = np.random.permutation(T).reshape(2, -1); r = np.random.randint(TOP, size=T // 2); x, y = deal[r, s_].copy(), deal[r, t_].copy()
        ok = ~((deal[:, s_] == y).any(0) | (deal[:, t_] == x).any(0)); deal[r[ok], s_[ok]] = y[ok]; deal[r[ok], t_[ok]] = x[ok]
    order = np.lexsort((np.random.rand(TOP * T), deal.reshape(-1)))
    slot_token = order % T; pos = np.empty(TOP * T, np.int64); pos[order] = np.arange(TOP * T); pos = pos.reshape(TOP, T)
    g = np.random.uniform(0.5, 1.5, (TOP, T)); g = g / g.sum(0)
    s = mx_kscale(E * C)[None, :]
    return {
        "hS": (n((K, E * C)) * s).astype(np.float32),
        "dyT": n((N, T)).astype(np.float32),
        "gate": np.tile(np.random.uniform(0.2, 1.0, E * C) / s, (N, 1)).astype(np.float32),
        "offs": striped(slot_token),
    }


def reference(hS, dyT, gate, offs):
    idx = unstriped(offs)
    hq = mxq(f64(hS), 1, "e4m3")
    gq = mxq(f64(gate) * f64(dyT)[:, idx], 1, "e4m3")
    return np.stack([(hq[:, e * C:(e + 1) * C] @ gq[:, e * C:(e + 1) * C].T) for e in range(E)])

from contextlib import ExitStack

import concourse.mybir as mybir
from concourse.masks import make_identity

K, T, E, C, N = 256, 1024, 6, 512, 128
FLOPS = 2 * E * K * C * N
BYTES = 4 * (K * E * C + N * T + E * C + E * K * N) + 2 * 128 * (E * C // 16)

F32 = mybir.dt.float32
BF16 = mybir.dt.bfloat16
U32 = mybir.dt.uint32
U16 = mybir.dt.uint16
U8 = mybir.dt.uint8
FP8X4 = mybir.dt.float8_e4m3fn_x4
COPY = mybir.ActivationFunctionType.Copy
MULT = mybir.AluOpType.mult

P = 128
KB = K // P
VECTOR_GATHERS = (2, 5)
CAST_ENGINES = "VVVVVS"
FLUSH_ENGINES = "SSSSSSS"
GROUPS = [[0], [1], [2], [3], [4]]
LAGS = [("Q", 5), ("Th", 3), ("D", 4), ("Tg", 2), ("B", 3), ("M", 10), ("F", 10), ("C", 1), ("G", 0)]


def tile_moe_lin_none_kernel(tc, hS, dyT, gate, offs, out):
    nc = tc.nc
    with ExitStack() as ctx:
        held = ctx.enter_context(tc.tile_pool(name="held", bufs=1))
        ring = ctx.enter_context(tc.tile_pool(name="ring", bufs=4))
        psum_g = ctx.enter_context(tc.psum_pool(name="psum_g", bufs=2))
        psum_h = ctx.enter_context(tc.psum_pool(name="psum_h", bufs=3))
        psum_o = ctx.enter_context(tc.psum_pool(name="psum_o", bufs=3))

        parts = {e: [(e, 0, KB)] for e in range(E - 1)}
        parts[E - 1] = [(E - 1, b, 1) for b in range(KB)]

        offsets = held.tile([P, E * C // 16], U16, name="offsets")
        nc.sync.dma_start(offsets[:], offs)
        dy = held.tile([P, T], F32, name="dy")
        nc.sync.dma_start(dy[:], dyT)

        gate_rows = held.tile([P, C], F32, name="gate_rows")
        nc.vector.memset(gate_rows[:], 0.0)
        gate_row = gate[0].rearrange("(e c) -> e c", e=E)
        nc.sync.dma_start(gate_rows[0:4, :], gate_row[0:4, :])
        nc.sync.dma_start(gate_rows[4:E, :], gate_row[4:E, :])

        h_rows = hS.rearrange("(k b) s -> k b s", b=KB)
        h_raw = {}
        for e in range(E):
            for part in parts[e]:
                b0, nb = part[1], part[2]
                h_raw[part] = held.tile([P, nb, C], F32, name="h_raw%d_%d" % (e, b0))
                nc.sync.dma_start(h_raw[part][:], h_rows[:, b0 : b0 + nb, e * C : (e + 1) * C])

        warm = held.tile([P, 1], F32, name="warm")
        cold = held.tile([P, 1], F32, name="cold")
        nc.gpsimd.memset(cold[:], 0.0)
        nc.scalar.activation(warm[:], cold[:], COPY)

        ident = held.tile([P, P], F32, name="ident")
        make_identity(nc, ident[:])

        gate_turned = psum_g.tile([P, 4, P], F32, name="gt")
        for t in range(4):
            nc.tensor.transpose(gate_turned[:, t, :], gate_rows[:, t:C:4], ident[:])
        gates = held.tile([P, E, 4], F32, name="gates")
        nc.vector.tensor_copy(gates[:], gate_turned[:, :, 0:E].rearrange("p t e -> p e t"))

        gathered, rounded, g_turned, h_turned, staged, quantised, sums = {}, {}, {}, {}, {}, {}, {}
        for e in range(E):
            for part in parts[e]:
                width = 4 * (part[2] * P + (N if part[1] == 0 else 0))
                staged[part] = held.tile([P, width], BF16, name="staged%d_%d" % (e, part[1]), align_bytes=64)

        def gather(e):
            looked_up = dy[:].indirect(offsets[:, e * (C // 16) : (e + 1) * (C // 16)])
            if e in VECTOR_GATHERS:
                g = ring.tile([P, C], F32, name="gathered_v")
                nc.vector.tensor_copy(g[:].rearrange("n (u p v) -> n p u v", u=2, v=2), looked_up)
                gathered[e] = [g[:, 256 * (t // 2) + t % 2 : 256 * (t // 2 + 1) : 2] for t in range(4)]
            else:
                g = ring.tile([P, C], F32, name="gathered_s")
                nc.scalar.activation(g[:], looked_up, COPY)
                gathered[e] = [g[:, t:C:4] for t in range(4)]

        def cast(e):
            for part in parts[e]:
                nb = part[2]
                hb = held.tile([P, nb * C], BF16, name="rounded%d_%d" % (e, part[1]))
                dst = hb[:].rearrange("k (b u p v) -> k b u p v", b=nb, u=2, v=2)
                src = h_raw[part][:].rearrange("k b (p u v) -> k b u p v", u=2, v=2)
                if CAST_ENGINES[e] == "S":
                    nc.scalar.copy(dst, src)
                elif CAST_ENGINES[e] == "G":
                    nc.gpsimd.tensor_copy(dst, src)
                else:
                    nc.vector.tensor_copy(dst, src)
                rounded[part] = hb

        def turn_g(e):
            gt = psum_g.tile([P, 4, N], F32, name="gt")
            for t in range(4):
                nc.tensor.transpose(gt[:, t, :], gathered[e][t], ident[:])
            g_turned[e] = gt

        def weigh(e):
            nc.vector.tensor_tensor(
                staged[parts[e][0]][:, : 4 * N].rearrange("p (n t) -> p n t", t=4),
                g_turned[e][:].rearrange("p t n -> p n t"),
                gates[:, e : e + 1, :].to_broadcast([P, N, 4]),
                MULT,
            )

        def turn_h(e):
            for part in parts[e]:
                nb = part[2]
                words = rounded[part][:].bitcast(F32)
                ht = psum_h.tile([P, nb, 2, P], F32, name="ht")
                for b in range(nb):
                    for u in range(2):
                        nc.tensor.transpose(ht[:, b, u, :], words[:, (2 * b + u) * P : (2 * b + u + 1) * P], ident[:])
                h_turned[part] = ht

        def weave(e):
            for part in parts[e]:
                first = 4 * N if part[1] == 0 else 0
                nc.scalar.copy(
                    staged[part][:, first:].bitcast(F32).rearrange("p (b k u) -> p b k u", b=part[2], u=2),
                    h_turned[part][:].rearrange("p b u k -> p b k u"),
                )

        def quantise(e):
            for part in parts[e]:
                width = staged[part].shape[1] // 4
                codes = held.tile([P, width], U32, name="codes%d_%d" % (e, part[1]), align_bytes=64)
                scales = held.tile([P, width], U8, name="scales%d_%d" % (e, part[1]), align_bytes=64)
                nc.vector.quantize_mx(out=codes[:].bitcast(FP8X4), scales=scales[:], in_=staged[part][:])
                quantised[part] = (codes, scales)

        def batches(e):
            if e == E - 1:
                return [[part] for part in parts[e]]
            return [[parts[x][0] for x in group] for group in GROUPS if group[-1] == e]

        def multiply(e):
            for batch in batches(e):
                acc = psum_o.tile([P, len(batch), batch[0][2], N], F32, name="acc")
                for i, part in enumerate(batch):
                    codes, scales = quantised[part]
                    g_codes, g_scales = quantised[parts[part[0]][0]]
                    first = N if part[1] == 0 else 0
                    for b in range(part[2]):
                        cols = slice(first + b * P, first + (b + 1) * P)
                        nc.tensor.matmul_mx(
                            out=acc[:, i, b, :],
                            lhsT=codes[:, cols].bitcast(FP8X4),
                            lhsT_scale=scales[:, cols],
                            rhs=g_codes[:, :N].bitcast(FP8X4),
                            rhs_scale=g_scales[:, :N],
                            start=True,
                            stop=True,
                        )
                sums[batch[0]] = acc

        def flush(e):
            for batch in batches(e):
                e0, b0, nb = batch[0]
                acc = sums[batch[0]]
                result = held.tile([P, len(batch), nb, N], F32, name="result%d_%d" % (e0, b0))
                if FLUSH_ENGINES[e0 + b0] == "S":
                    nc.scalar.copy(result[:], acc[:])
                else:
                    nc.vector.tensor_copy(result[:], acc[:])
                rows = out[e0 : e0 + len(batch)].rearrange("e (k b) n -> k e b n", b=KB)
                queue = nc.scalar if b0 == KB - 1 else nc.sync
                queue.dma_start(rows[:, :, b0 : b0 + nb, :], result[:])

        stages = {"G": gather, "C": cast, "Tg": turn_g, "B": weigh, "Th": turn_h, "D": weave, "Q": quantise, "M": multiply, "F": flush}
        for step in range(E + max(lag for name, lag in LAGS)):
            for name, lag in LAGS:
                if 0 <= step - lag < E:
                    stages[name](step - lag)
